import numpy as np
import ml_dtypes


def mxq(x, axis, fmt="e4m3"):
    dtype, down = {"e4m3": (ml_dtypes.float8_e4m3fn, 7), "e5m2": (ml_dtypes.float8_e5m2, 14)}[fmt]
    v = np.moveaxis(np.asarray(x, np.float32).astype(ml_dtypes.bfloat16).astype(np.float64), axis, -1)
    blocks = v.reshape(v.shape[:-1] + (-1, 32))
    amax = np.abs(blocks).max(-1, keepdims=True)
    byte = np.maximum(np.where(amax > 0, np.frexp(amax)[1] - 1 + 127, 0) - down, 1)
    scale = np.exp2(byte - 127.0)
    codes = (blocks / scale).astype(np.float32).astype(dtype).astype(np.float64)
    return np.moveaxis((codes * scale).reshape(v.shape), -1, axis)


WIDE = False


def mx_kscale(k):
    if not WIDE:
        return np.ones(k)
    levels = np.array([30, -30])
    if k % 512:
        return np.exp2(np.random.permutation(np.resize(levels, k // 32))).repeat(32)
    a = np.empty((k // 512, 16))
    for p in range(k // 512):
        a[p, :8] = np.random.permutation(np.resize(levels, 8))
        for g in range(8):
            far = levels[np.abs(levels - a[p, g]) >= 10]
            a[p, g + 8] = far[np.random.randint(len(far))]
    return np.exp2(a.ravel()).repeat(32)


def f64(x):
    return np.asarray(x).astype(np.float64)


E2M1 = np.array([0.0, 0.5, 1.0, 1.5, 2.0, 3.0, 4.0, 6.0, -0.0, -0.5, -1.0, -1.5, -2.0, -3.0, -4.0, -6.0])


def pack_weight(w, fmt):
    k, n = w.shape
    w = f64(np.asarray(w, np.float32).astype(ml_dtypes.bfloat16)).reshape(k // 32, 32, n)
    amax = np.abs(w).max(1)
    if fmt == "e4m3":
        byte = np.frexp(amax)[1] - 1 + 127 - 7
    else:
        mant, ex = np.frexp(amax / 6.0)
        byte = np.where(mant > 0.5, ex, ex - 1) + 127
    byte = np.clip(np.where(amax > 0, byte, 1), 1, 254)
    scaled = (w * np.exp2(127.0 - byte)[:, None, :]).reshape(k, n).astype(np.float32)
    by_word = np.ascontiguousarray(scaled.reshape(k // 512, 128, 4, n).transpose(0, 1, 3, 2))
    if fmt == "e4m3":
        words = by_word.astype(ml_dtypes.float8_e4m3fn).view(np.uint8)
    else:
        c = by_word.astype(ml_dtypes.float4_e2m1fn).view(np.uint8) & 0xF
        words = (c[..., 0::2] | (c[..., 1::2] << 4)).reshape(k // 512, 128, 2 * n)
    return np.ascontiguousarray(words), np.ascontiguousarray(byte.astype(np.uint8).reshape(k // 512, 16, n))


def unpack_weight(words, scales, fmt):
    g, _, n = scales.shape
    words = np.ascontiguousarray(words).reshape(g, 128, n, -1)
    if fmt == "e4m3":
        vals = words.view(ml_dtypes.float8_e4m3fn).astype(np.float64)
    else:
        nib = np.empty((g, 128, n, 4), np.uint8)
        nib[..., 0::2] = words & 0xF
        nib[..., 1::2] = words >> 4
        vals = E2M1[nib]
    vals = vals * np.repeat(np.exp2(scales.astype(np.float64) - 127.0), 8, axis=1)[..., None]
    return vals.transpose(0, 1, 3, 2).reshape(g * 512, n)


def gelu(v):
    return 0.5 * v * (1.0 + np.tanh(np.sqrt(2.0 / np.pi) * (v + 0.044715 * v**3)))


K, L, R, M, T = 1536, 1024, 1024, 1536, 512


def setup_inputs():
    n = np.random.standard_normal
    s1 = mx_kscale(K)[:, None]
    s2 = mx_kscale(L)[:, None]
    u = mx_kscale(R)[:, None]
    p_w = pack_weight(n((R, M)) / np.sqrt(R) / u, "e2m1")
    return {
        "x": (n((K, T)) * s1).astype(np.float32),
        "wx": (n((K, R)) / np.sqrt(K) / s1 * u.T).astype(np.float32),
        "c": (n((L, T)) * s2).astype(np.float32),
        "wc": (n((L, R)) / np.sqrt(L) / s2).astype(np.float32),
        "w_words": p_w[0],
        "w_scales": p_w[1],
        "b": (0.3 * n(1536)).astype(np.float32),
    }


def reference(x, wx, c, wc, w_words, w_scales, b):
    x_ = mxq(f64(x), 0, "e4m3")
    wx_ = mxq(f64(wx), 0, "e4m3")
    c_ = mxq(f64(c), 0, "e5m2")
    wc_ = mxq(f64(wc), 0, "e4m3")
    w_ = unpack_weight(w_words, w_scales, "e2m1")
    h_ = mxq((wx_.T @ x_) * (wc_.T @ c_), 0, "e4m3")
    y = w_.T @ h_
    return gelu(y + f64(b)[:, None])

@@ -1,0 +1,222 @@
+from contextlib import ExitStack
+
+import concourse.mybir as mybir
+from concourse.masks import make_identity
+
+K, L, R, M, T = 1536, 1024, 1024, 1536, 512
+FLOPS = 2 * T * (K * R + L * R + R * M)
+
+F32 = mybir.dt.float32
+BF16 = mybir.dt.bfloat16
+I32 = mybir.dt.int32
+U32 = mybir.dt.uint32
+U8 = mybir.dt.uint8
+E4M3 = mybir.dt.float8_e4m3fn_x4
+E5M2 = mybir.dt.float8_e5m2_x4
+E2M1 = mybir.dt.float4_e2m1fn_x4
+GELU = mybir.ActivationFunctionType.Gelu_apprx_tanh
+
+P = 128
+PACK = 4
+PASS = P * PACK
+TQ = 128
+QUARTERS = T // TQ
+N_TILES = M // P
+W_GROUP = 4
+VECTOR_TOKENS = 320
+VECTOR_ROWS = 72
+VECTOR_ROWS_LAST = 44
+EARLY_TILES = 4
+
+
+def tile_mix_bilin_fm_gelu_kernel(tc, x, wx, c, wc, w_words, w_scales, b, out):
+    nc = tc.nc
+    with ExitStack() as ctx:
+        keep = ctx.enter_context(tc.tile_pool(name="keep", bufs=1))
+        work = ctx.enter_context(tc.tile_pool(name="work", bufs=3))
+        psum = ctx.enter_context(tc.psum_pool(name="psum", bufs=8))
+        ctx.enter_context(tc.manual_schedule())
+
+        def load(name, src, g, col0, width):
+            raw = keep.tile([P, PACK, width], F32, name=name)
+            rows = src[g * PASS : (g + 1) * PASS, col0 : col0 + width]
+            nc.sync.dma_start(out=raw[:], in_=rows.rearrange("(p j) n -> p j n", j=PACK))
+            return raw
+
+        b_rows = keep.tile([P, P], F32, name="b_rows")
+        ident = keep.tile([P, P], F32, name="ident")
+        bias = keep.tile([P, N_TILES], F32, name="bias")
+        w_plane = keep.tile([P, 2, M], U8, name="w_plane", align_bytes=64)
+        nc.vector.memset(b_rows[:], 0.0)
+        nc.vector.memset(w_plane[:].bitcast(I32), 0)
+        make_identity(nc, ident[:])
+
+        c_raw = [load("c_raw%d" % g, c, g, 0, T) for g in range(2)]
+        nc.sync.dma_start(out=b_rows[0:N_TILES, :], in_=b.rearrange("(i p) -> i p", p=P))
+        wc_raw = {(0, g): load("wc_raw0%d" % g, wc, g, 0, PASS) for g in range(2)}
+        x_raw = [load("x_raw%d" % g, x, g, 0, T) for g in range(3)]
+        wx_raw = {(0, g): load("wx_raw0%d" % g, wx, g, 0, PASS) for g in range(3)}
+        wc_raw.update({(1, g): load("wc_raw1%d" % g, wc, g, PASS, PASS) for g in range(2)})
+        wx_raw.update({(1, g): load("wx_raw1%d" % g, wx, g, PASS, PASS) for g in range(2)})
+        last_raw = [load("last_raw%d" % s, wx, 2, PASS + s * 256, 256) for s in range(2)]
+        for r in range(4):
+            nc.sync.dma_start(
+                out=w_plane[r:P:32, :, :].bitcast(I32),
+                in_=w_scales[:, r:16:4, :].rearrange("a q n -> q a n").bitcast(I32),
+            )
+        w_codes = []
+        for k in range(N_TILES // W_GROUP):
+            part = keep.tile([P, 2, 2 * P * W_GROUP], U8, name="w_codes%d" % k, align_bytes=64)
+            cols = slice(2 * P * W_GROUP * k, 2 * P * W_GROUP * (k + 1))
+            nc.sync.dma_start(
+                out=part[:].bitcast(I32),
+                in_=w_words[:, :, cols].rearrange("a p n -> p a n").bitcast(I32),
+            )
+            w_codes.append(part)
+
+        def group_stream(raw):
+            grouped = work.tile([P, T, PACK], BF16, name="grouped", align_bytes=64)
+            for copy, cols in (
+                (nc.vector.tensor_copy, slice(0, VECTOR_TOKENS)),
+                (nc.scalar.copy, slice(VECTOR_TOKENS, T)),
+            ):
+                copy(
+                    out=grouped[:, cols, :].rearrange("p (n i) j -> p n j i", i=4),
+                    in_=raw[:, :, cols].rearrange("p j (n i) -> p n j i", i=4),
+                )
+            return grouped[:].rearrange("p n j -> p (n j)")
+
+        def group_weight(parts, share):
+            grouped = work.tile([P, T, PACK], BF16, name="grouped", align_bytes=64)
+            view = grouped[:].rearrange("p (t m) j -> p m j t", t=PACK)
+            rows = P // len(parts)
+            for s, raw in enumerate(parts):
+                src = raw[:].rearrange("p j (m t) -> p m j t", t=PACK)
+                nc.vector.tensor_copy(out=view[:, s * rows : s * rows + share], in_=src[:, 0:share])
+                nc.scalar.copy(out=view[:, s * rows + share : (s + 1) * rows], in_=src[:, share:rows])
+            return grouped[:].rearrange("p n j -> p (n j)")
+
+        def quantize(pool, name, grouped, fmt):
+            codes = pool.tile([P, PASS], U32, name=name + "_codes", align_bytes=64)
+            plane = pool.tile([P, PASS], U8, name=name + "_plane", align_bytes=64)
+            nc.vector.quantize_mx(out=codes[:].bitcast(fmt), scales=plane[:], in_=grouped)
+            return codes, plane
+
+        def project(banks, weight, stream, fmt, first, last):
+            for q in range(QUARTERS):
+                tok = slice(q * TQ, (q + 1) * TQ)
+                for t in range(PACK):
+                    cols = slice(t * P, (t + 1) * P)
+                    nc.tensor.matmul_mx(
+                        out=banks[q][:, cols],
+                        lhsT=weight[0][:, cols].bitcast(E4M3),
+                        lhsT_scale=weight[1][:, cols],
+                        rhs=stream[0][:, tok].bitcast(fmt),
+                        rhs_scale=stream[1][:, tok],
+                        start=first and t == 0,
+                        stop=last and t == PACK - 1,
+                    )
+
+        def new_banks():
+            return [psum.tile([P, T], F32, name="bank") for q in range(QUARTERS)]
+
+        pc_sb = [keep.tile([P, T * PACK], F32, name="pc_sb%d" % a) for a in range(2)]
+        h_bf = [keep.tile([P, T * PACK], BF16, name="h_bf%d" % a, align_bytes=64) for a in range(2)]
+        h_codes = [keep.tile([P, T], U32, name="h_codes%d" % a, align_bytes=64) for a in range(2)]
+        h_plane = [keep.tile([P, T], U8, name="h_plane%d" % a, align_bytes=64) for a in range(2)]
+
+        def drain_pc(a, q, bank):
+            nc.scalar.copy(
+                out=pc_sb[a][:, q * PASS : (q + 1) * PASS].rearrange("p (n t) -> p n t", t=PACK),
+                in_=bank[:].rearrange("p (t n) -> p n t", t=PACK),
+            )
+
+        def multiply(a, q, bank):
+            cols = slice(q * PASS, (q + 1) * PASS)
+            nc.vector.tensor_tensor(
+                out=h_bf[a][:, cols].rearrange("p (n t) -> p n t", t=PACK),
+                in0=bank[:].rearrange("p (t n) -> p n t", t=PACK),
+                in1=pc_sb[a][:, cols].rearrange("p (n t) -> p n t", t=PACK),
+                op=mybir.AluOpType.mult,
+            )
+
+        def quantize_h(a, q0, q1):
+            tok = slice(q0 * TQ, q1 * TQ)
+            nc.vector.quantize_mx(
+                out=h_codes[a][:, tok].bitcast(E4M3),
+                scales=h_plane[a][:, tok],
+                in_=h_bf[a][:, q0 * PASS : q1 * PASS],
+            )
+
+        c_q = [quantize(keep, "c%d" % g, group_stream(c_raw[g]), E5M2) for g in range(2)]
+        b_bank = psum.tile([P, T], F32, name="bank")
+        nc.tensor.transpose(b_bank[:, 0:P], b_rows[:], ident[:])
+        nc.vector.tensor_copy(out=bias[:], in_=b_bank[:, 0:N_TILES])
+        pc = new_banks()
+        for g in range(2):
+            wq = quantize(work, "wt", group_weight([wc_raw[0, g]], VECTOR_ROWS), E4M3)
+            project(pc, wq, c_q[g], E5M2, g == 0, g == 1)
+        x_q = []
+        for g in range(3):
+            x_q.append(quantize(keep, "x%d" % g, group_stream(x_raw[g]), E4M3))
+            for q in range(QUARTERS):
+                if q // 2 == g:
+                    drain_pc(0, q, pc[q])
+        px = new_banks()
+        for g in range(3):
+            wq = quantize(work, "wt", group_weight([wx_raw[0, g]], VECTOR_ROWS), E4M3)
+            project(px, wq, x_q[g], E4M3, g == 0, g == 2)
+
+        pc = new_banks()
+        px_first = px
+        for g in range(2):
+            grouped = group_weight([wc_raw[1, g]], VECTOR_ROWS)
+            multiply(0, 2 * g, px_first[2 * g])
+            wq = quantize(work, "wt", grouped, E4M3)
+            multiply(0, 2 * g + 1, px_first[2 * g + 1])
+            project(pc, wq, c_q[g], E5M2, g == 0, g == 1)
+        px = new_banks()
+        for g in range(3):
+            if g < 2:
+                grouped = group_weight([wx_raw[1, g]], VECTOR_ROWS)
+                quantize_h(0, 2 * g, 2 * g + 2)
+                drain_pc(1, 2 * g, pc[2 * g])
+                drain_pc(1, 2 * g + 1, pc[2 * g + 1])
+            else:
+                grouped = group_weight(last_raw, VECTOR_ROWS_LAST)
+            wq = quantize(work, "wt", grouped, E4M3)
+            project(px, wq, x_q[g], E4M3, g == 0, g == 2)
+
+        result = [keep.tile([P, T], F32, name="result%d" % i) for i in range(N_TILES)]
+
+        def finish(i, t0, t1):
+            tok = slice(t0, t1)
+            bank = psum.tile([P, T], F32, name="bank")
+            k, ii = divmod(i, W_GROUP)
+            for a in range(2):
+                nc.tensor.matmul_mx(
+                    out=bank[:, tok],
+                    lhsT=w_codes[k][:, a, 2 * P * ii : 2 * P * (ii + 1)].bitcast(E2M1),
+                    lhsT_scale=w_plane[:, a, P * i : P * (i + 1)],
+                    rhs=h_codes[a][:, tok].bitcast(E4M3),
+                    rhs_scale=h_plane[a][:, tok],
+                    start=a == 0,
+                    stop=a == 1,
+                )
+            nc.scalar.activation(out=result[i][:, tok], in_=bank[:, tok], func=GELU, bias=bias[:, i : i + 1])
+            nc.sync.dma_start(out=out[i * P : (i + 1) * P, tok], in_=result[i][:, tok])
+
+        multiply(1, 0, px[0])
+        multiply(1, 1, px[1])
+        quantize_h(1, 0, 1)
+        quantize_h(1, 1, 2)
+        for i in range(EARLY_TILES):
+            finish(i, 0, T // 2)
+        multiply(1, 2, px[2])
+        multiply(1, 3, px[3])
+        quantize_h(1, 2, 3)
+        quantize_h(1, 3, 4)
+        for i in range(EARLY_TILES):
+            finish(i, T // 2, T)
+        for i in range(EARLY_TILES, N_TILES):
+            finish(i, 0, T)

@@ -81,8 +81,8 @@ def tile_mix_bilin_fm_gelu_kernel(tc, x, wx, c, wc, w_words, w_scales, b, out):
                 (nc.scalar.copy, slice(VECTOR_TOKENS, T)),
             ):
                 copy(
-                    out=grouped[:, cols, :].rearrange("p (n i) j -> p n j i", i=4),
-                    in_=raw[:, :, cols].rearrange("p j (n i) -> p n j i", i=4),
+                    out=grouped[:, cols, :].rearrange("p (n i) j -> p n j i", i=2),
+                    in_=raw[:, :, cols].rearrange("p j (n i) -> p n j i", i=2),
                 )
             return grouped[:].rearrange("p n j -> p (n j)")
 
@@ -92,30 +92,44 @@ def tile_mix_bilin_fm_gelu_kernel(tc, x, wx, c, wc, w_words, w_scales, b, out):
             rows = P // len(parts)
             for s, raw in enumerate(parts):
                 src = raw[:].rearrange("p j (m t) -> p m j t", t=PACK)
-                nc.vector.tensor_copy(out=view[:, s * rows : s * rows + share], in_=src[:, 0:share])
-                nc.scalar.copy(out=view[:, s * rows + share : (s + 1) * rows], in_=src[:, share:rows])
+                for u in range(2):
+                    pair = slice(2 * u, 2 * u + 2)
+                    nc.vector.tensor_copy(
+                        out=view[:, s * rows : s * rows + share, :, pair], in_=src[:, 0:share, :, pair]
+                    )
+                    nc.scalar.copy(
+                        out=view[:, s * rows + share : (s + 1) * rows, :, pair], in_=src[:, share:rows, :, pair]
+                    )
             return grouped[:].rearrange("p n j -> p (n j)")
 
-        def quantize(pool, name, grouped, fmt):
+        def quantize(pool, name, grouped, fmt, calls=1):
             codes = pool.tile([P, PASS], U32, name=name + "_codes", align_bytes=64)
             plane = pool.tile([P, PASS], U8, name=name + "_plane", align_bytes=64)
-            nc.vector.quantize_mx(out=codes[:].bitcast(fmt), scales=plane[:], in_=grouped)
+            width = PASS // calls
+            for u in range(calls):
+                cols = slice(u * width, (u + 1) * width)
+                nc.vector.quantize_mx(
+                    out=codes[:, cols].bitcast(fmt),
+                    scales=plane[:, cols],
+                    in_=grouped[:, u * width * PACK : (u + 1) * width * PACK],
+                )
             return codes, plane
 
         def project(banks, weight, stream, fmt, first, last):
-            for q in range(QUARTERS):
-                tok = slice(q * TQ, (q + 1) * TQ)
-                for t in range(PACK):
-                    cols = slice(t * P, (t + 1) * P)
-                    nc.tensor.matmul_mx(
-                        out=banks[q][:, cols],
-                        lhsT=weight[0][:, cols].bitcast(E4M3),
-                        lhsT_scale=weight[1][:, cols],
-                        rhs=stream[0][:, tok].bitcast(fmt),
-                        rhs_scale=stream[1][:, tok],
-                        start=first and t == 0,
-                        stop=last and t == PACK - 1,
-                    )
+            for u in range(2):
+                for q in range(QUARTERS):
+                    tok = slice(q * TQ, (q + 1) * TQ)
+                    for t in range(2 * u, 2 * u + 2):
+                        cols = slice(t * P, (t + 1) * P)
+                        nc.tensor.matmul_mx(
+                            out=banks[q][:, cols],
+                            lhsT=weight[0][:, cols].bitcast(E4M3),
+                            lhsT_scale=weight[1][:, cols],
+                            rhs=stream[0][:, tok].bitcast(fmt),
+                            rhs_scale=stream[1][:, tok],
+                            start=first and t == 0,
+                            stop=last and t == PACK - 1,
+                        )
 
         def new_banks():
             return [psum.tile([P, T], F32, name="bank") for q in range(QUARTERS)]
@@ -184,7 +198,7 @@ def tile_mix_bilin_fm_gelu_kernel(tc, x, wx, c, wc, w_words, w_scales, b, out):
                 drain_pc(1, 2 * g + 1, pc[2 * g + 1])
             else:
                 grouped = group_weight(last_raw, VECTOR_ROWS_LAST)
-            wq = quantize(work, "wt", grouped, E4M3)
+            wq = quantize(work, "wt", grouped, E4M3, 2 if g == 2 else 1)
             project(px, wq, x_q[g], E4M3, g == 0, g == 2)
 
         result = [keep.tile([P, T], F32, name="result%d" % i) for i in range(N_TILES)]

@@ -19,14 +19,18 @@ GELU = mybir.ActivationFunctionType.Gelu_apprx_tanh
 P = 128
 PACK = 4
 PASS = P * PACK
-TQ = 128
-QUARTERS = T // TQ
+QUARTER = 128
+QUARTERS = T // QUARTER
+HALF = T // 2
 N_TILES = M // P
-W_GROUP = 4
+W_PARTS = (4, 8)
 VECTOR_TOKENS = 320
-VECTOR_ROWS = 72
-VECTOR_ROWS_LAST = 44
-EARLY_TILES = 4
+VECTOR_GROUPS = 80
+VECTOR_GROUPS_BUSY = 64
+VECTOR_GROUPS_LAST = (24, 44)
+FIRST_HALF_STORES = (1, 1, 2, 4)
+SECOND_HALF_STORES = (4, 4)
+WHOLE_STORES = (2, 1, 1)
 
 
 def tile_mix_bilin_fm_gelu_kernel(tc, x, wx, c, wc, w_words, w_scales, b, out):
@@ -34,7 +38,7 @@ def tile_mix_bilin_fm_gelu_kernel(tc, x, wx, c, wc, w_words, w_scales, b, out):
     with ExitStack() as ctx:
         keep = ctx.enter_context(tc.tile_pool(name="keep", bufs=1))
         work = ctx.enter_context(tc.tile_pool(name="work", bufs=3))
-        psum = ctx.enter_context(tc.psum_pool(name="psum", bufs=8))
+        psum = ctx.enter_context(tc.psum_pool(name="psum", bufs=4))
         ctx.enter_context(tc.manual_schedule())
 
         def load(name, src, g, col0, width):
@@ -42,6 +46,10 @@ def tile_mix_bilin_fm_gelu_kernel(tc, x, wx, c, wc, w_words, w_scales, b, out):
             rows = src[g * PASS : (g + 1) * PASS, col0 : col0 + width]
             nc.sync.dma_start(out=raw[:], in_=rows.rearrange("(p j) n -> p j n", j=PACK))
             return raw
+
+        def load_both_halves(name, src, g):
+            raw = load(name, src, g, 0, R)
+            return [raw[:, :, a * PASS : (a + 1) * PASS] for a in range(2)]
 
         b_rows = keep.tile([P, P], F32, name="b_rows")
         ident = keep.tile([P, P], F32, name="ident")
@@ -53,53 +61,49 @@ def tile_mix_bilin_fm_gelu_kernel(tc, x, wx, c, wc, w_words, w_scales, b, out):
 
         c_raw = [load("c_raw%d" % g, c, g, 0, T) for g in range(2)]
         nc.sync.dma_start(out=b_rows[0:N_TILES, :], in_=b.rearrange("(i p) -> i p", p=P))
-        wc_raw = {(0, g): load("wc_raw0%d" % g, wc, g, 0, PASS) for g in range(2)}
+        wc_raw = [load_both_halves("wc_raw%d" % g, wc, g) for g in range(2)]
         x_raw = [load("x_raw%d" % g, x, g, 0, T) for g in range(3)]
-        wx_raw = {(0, g): load("wx_raw0%d" % g, wx, g, 0, PASS) for g in range(3)}
-        wc_raw.update({(1, g): load("wc_raw1%d" % g, wc, g, PASS, PASS) for g in range(2)})
-        wx_raw.update({(1, g): load("wx_raw1%d" % g, wx, g, PASS, PASS) for g in range(2)})
-        last_raw = [load("last_raw%d" % s, wx, 2, PASS + s * 256, 256) for s in range(2)]
-        for r in range(4):
+        wx_first = load_both_halves("wx_raw0", wx, 0)
+        wx_raw = {(a, 0): wx_first[a] for a in range(2)}
+        for a, g in ((0, 1), (0, 2), (1, 1)):
+            wx_raw[a, g] = load("wx_raw%d%d" % (a, g), wx, g, a * PASS, PASS)[:]
+        last_raw = [load("last_raw%d" % s, wx, 2, PASS + s * PASS // 2, PASS // 2) for s in range(2)]
+        for quad in range(4):
             nc.sync.dma_start(
-                out=w_plane[r:P:32, :, :].bitcast(I32),
-                in_=w_scales[:, r:16:4, :].rearrange("a q n -> q a n").bitcast(I32),
+                out=w_plane[32 * quad : 32 * quad + 4, :, :].bitcast(I32),
+                in_=w_scales[:, 4 * quad : 4 * quad + 4, :].rearrange("a r n -> r a n").bitcast(I32),
             )
         w_codes = []
-        for k in range(N_TILES // W_GROUP):
-            part = keep.tile([P, 2, 2 * P * W_GROUP], U8, name="w_codes%d" % k, align_bytes=64)
-            cols = slice(2 * P * W_GROUP * k, 2 * P * W_GROUP * (k + 1))
+        for tiles in W_PARTS:
+            first = len(w_codes)
+            part = keep.tile([P, 2, 2 * P * tiles], U8, name="w_codes%d" % first, align_bytes=64)
             nc.sync.dma_start(
                 out=part[:].bitcast(I32),
-                in_=w_words[:, :, cols].rearrange("a p n -> p a n").bitcast(I32),
+                in_=w_words[:, :, 2 * P * first : 2 * P * (first + tiles)].rearrange("a p n -> p a n").bitcast(I32),
             )
-            w_codes.append(part)
+            w_codes.extend(part[:, :, 2 * P * i : 2 * P * (i + 1)] for i in range(tiles))
 
-        def group_stream(raw):
+        def group_stream(raw, share):
             grouped = work.tile([P, T, PACK], BF16, name="grouped", align_bytes=64)
-            for copy, cols in (
-                (nc.vector.tensor_copy, slice(0, VECTOR_TOKENS)),
-                (nc.scalar.copy, slice(VECTOR_TOKENS, T)),
-            ):
-                copy(
-                    out=grouped[:, cols, :].rearrange("p (n i) j -> p n j i", i=2),
-                    in_=raw[:, :, cols].rearrange("p j (n i) -> p n j i", i=2),
-                )
+            dst = grouped[:].rearrange("p (n i) j -> p n j i", i=2)
+            src = raw[:].rearrange("p j (n i) -> p n j i", i=2)
+            nc.vector.tensor_copy(out=dst[:, 0 : share // 2], in_=src[:, 0 : share // 2])
+            if share < T:
+                nc.scalar.copy(out=dst[:, share // 2 :], in_=src[:, share // 2 :])
             return grouped[:].rearrange("p n j -> p (n j)")
 
-        def group_weight(parts, share):
-            grouped = work.tile([P, T, PACK], BF16, name="grouped", align_bytes=64)
-            view = grouped[:].rearrange("p (t m) j -> p m j t", t=PACK)
-            rows = P // len(parts)
-            for s, raw in enumerate(parts):
-                src = raw[:].rearrange("p j (m t) -> p m j t", t=PACK)
-                for u in range(2):
-                    pair = slice(2 * u, 2 * u + 2)
-                    nc.vector.tensor_copy(
-                        out=view[:, s * rows : s * rows + share, :, pair], in_=src[:, 0:share, :, pair]
-                    )
-                    nc.scalar.copy(
-                        out=view[:, s * rows + share : (s + 1) * rows, :, pair], in_=src[:, share:rows, :, pair]
-                    )
+        def group_columns(grouped, first, raw, share):
+            src = raw.rearrange("p j (m t) -> p m j t", t=PACK)
+            groups = src.shape[1]
+            dst = grouped[:].rearrange("p (t m) j -> p m j t", t=PACK)[:, first : first + groups]
+            for u in range(2):
+                pair = slice(2 * u, 2 * u + 2)
+                nc.vector.tensor_copy(out=dst[:, 0:share, :, pair], in_=src[:, 0:share, :, pair])
+                nc.scalar.copy(out=dst[:, share:, :, pair], in_=src[:, share:, :, pair])
+
+        def group_weight(raw, share):
+            grouped = work.tile([P, PASS, PACK], BF16, name="grouped", align_bytes=64)
+            group_columns(grouped, 0, raw, share)
             return grouped[:].rearrange("p n j -> p (n j)")
 
         def quantize(pool, name, grouped, fmt, calls=1):
@@ -115,122 +119,121 @@ def tile_mix_bilin_fm_gelu_kernel(tc, x, wx, c, wc, w_words, w_scales, b, out):
                 )
             return codes, plane
 
-        def project(banks, weight, stream, fmt, first, last):
-            for u in range(2):
-                for q in range(QUARTERS):
-                    tok = slice(q * TQ, (q + 1) * TQ)
-                    for t in range(2 * u, 2 * u + 2):
-                        cols = slice(t * P, (t + 1) * P)
-                        nc.tensor.matmul_mx(
-                            out=banks[q][:, cols],
-                            lhsT=weight[0][:, cols].bitcast(E4M3),
-                            lhsT_scale=weight[1][:, cols],
-                            rhs=stream[0][:, tok].bitcast(fmt),
-                            rhs_scale=stream[1][:, tok],
-                            start=first and t == 0,
-                            stop=last and t == PACK - 1,
-                        )
+        def project(banks, weight, stream, fmt, first, last, order):
+            for q, t in order:
+                tok = slice(q * QUARTER, (q + 1) * QUARTER)
+                cols = slice(t * P, (t + 1) * P)
+                nc.tensor.matmul_mx(
+                    out=banks[q][:, cols],
+                    lhsT=weight[0][:, cols].bitcast(E4M3),
+                    lhsT_scale=weight[1][:, cols],
+                    rhs=stream[0][:, tok].bitcast(fmt),
+                    rhs_scale=stream[1][:, tok],
+                    start=first and t == 0,
+                    stop=last and t == PACK - 1,
+                )
+
+        plain = [(q, t) for q in range(QUARTERS) for t in range(PACK)]
+        urgent = [(q, 2 * u + t) for u in range(2) for q in range(2) for t in range(2)] + plain[2 * PACK :]
 
         def new_banks():
-            return [psum.tile([P, T], F32, name="bank") for q in range(QUARTERS)]
+            return [psum.tile([P, PASS], F32, name="bank%d" % (q // 2)) for q in range(QUARTERS)]
 
         pc_sb = [keep.tile([P, T * PACK], F32, name="pc_sb%d" % a) for a in range(2)]
         h_bf = [keep.tile([P, T * PACK], BF16, name="h_bf%d" % a, align_bytes=64) for a in range(2)]
         h_codes = [keep.tile([P, T], U32, name="h_codes%d" % a, align_bytes=64) for a in range(2)]
         h_plane = [keep.tile([P, T], U8, name="h_plane%d" % a, align_bytes=64) for a in range(2)]
 
-        def drain_pc(a, q, bank):
+        def drain_pc(a, q):
             nc.scalar.copy(
                 out=pc_sb[a][:, q * PASS : (q + 1) * PASS].rearrange("p (n t) -> p n t", t=PACK),
-                in_=bank[:].rearrange("p (t n) -> p n t", t=PACK),
+                in_=pc[a][q][:].rearrange("p (t n) -> p n t", t=PACK),
             )
 
-        def multiply(a, q, bank):
+        def multiply(a, q):
             cols = slice(q * PASS, (q + 1) * PASS)
             nc.vector.tensor_tensor(
                 out=h_bf[a][:, cols].rearrange("p (n t) -> p n t", t=PACK),
-                in0=bank[:].rearrange("p (t n) -> p n t", t=PACK),
+                in0=px[a][q][:].rearrange("p (t n) -> p n t", t=PACK),
                 in1=pc_sb[a][:, cols].rearrange("p (n t) -> p n t", t=PACK),
                 op=mybir.AluOpType.mult,
             )
 
         def quantize_h(a, q0, q1):
-            tok = slice(q0 * TQ, q1 * TQ)
+            tok = slice(q0 * QUARTER, q1 * QUARTER)
             nc.vector.quantize_mx(
                 out=h_codes[a][:, tok].bitcast(E4M3),
                 scales=h_plane[a][:, tok],
                 in_=h_bf[a][:, q0 * PASS : q1 * PASS],
             )
 
-        c_q = [quantize(keep, "c%d" % g, group_stream(c_raw[g]), E5M2) for g in range(2)]
-        b_bank = psum.tile([P, T], F32, name="bank")
+        def finish(first, stores, tok, tags):
+            width = tok.stop - tok.start
+            for tiles in stores:
+                result = keep.tile([P, tiles, width], F32, name="result%d_%d" % (first, tok.start))
+                for i in range(first, first + tiles):
+                    bank = psum.tile([P, PASS], F32, name="bank%d" % tags[i % len(tags)])
+                    for a in range(2):
+                        nc.tensor.matmul_mx(
+                            out=bank[:, 0:width],
+                            lhsT=w_codes[i][:, a, :].bitcast(E2M1),
+                            lhsT_scale=w_plane[:, a, P * i : P * (i + 1)],
+                            rhs=h_codes[a][:, tok].bitcast(E4M3),
+                            rhs_scale=h_plane[a][:, tok],
+                            start=a == 0,
+                            stop=a == 1,
+                        )
+                    nc.scalar.activation(
+                        out=result[:, i - first, :], in_=bank[:, 0:width], func=GELU, bias=bias[:, i : i + 1]
+                    )
+                rows = out[first * P : (first + tiles) * P, tok]
+                nc.sync.dma_start(out=rows.rearrange("(i p) n -> p i n", p=P), in_=result[:])
+                first += tiles
+
+        c_q = [quantize(keep, "c%d" % g, group_stream(c_raw[g], VECTOR_TOKENS), E5M2) for g in range(2)]
+        b_bank = psum.tile([P, PASS], F32, name="bank0")
         nc.tensor.transpose(b_bank[:, 0:P], b_rows[:], ident[:])
         nc.vector.tensor_copy(out=bias[:], in_=b_bank[:, 0:N_TILES])
-        pc = new_banks()
+        pc = [new_banks() for a in range(2)]
         for g in range(2):
-            wq = quantize(work, "wt", group_weight([wc_raw[0, g]], VECTOR_ROWS), E4M3)
-            project(pc, wq, c_q[g], E5M2, g == 0, g == 1)
-        x_q = []
-        for g in range(3):
-            x_q.append(quantize(keep, "x%d" % g, group_stream(x_raw[g]), E4M3))
-            for q in range(QUARTERS):
-                if q // 2 == g:
-                    drain_pc(0, q, pc[q])
-        px = new_banks()
-        for g in range(3):
-            wq = quantize(work, "wt", group_weight([wx_raw[0, g]], VECTOR_ROWS), E4M3)
-            project(px, wq, x_q[g], E4M3, g == 0, g == 2)
-
-        pc = new_banks()
-        px_first = px
-        for g in range(2):
-            grouped = group_weight([wc_raw[1, g]], VECTOR_ROWS)
-            multiply(0, 2 * g, px_first[2 * g])
-            wq = quantize(work, "wt", grouped, E4M3)
-            multiply(0, 2 * g + 1, px_first[2 * g + 1])
-            project(pc, wq, c_q[g], E5M2, g == 0, g == 1)
-        px = new_banks()
-        for g in range(3):
-            if g < 2:
-                grouped = group_weight([wx_raw[1, g]], VECTOR_ROWS)
-                quantize_h(0, 2 * g, 2 * g + 2)
-                drain_pc(1, 2 * g, pc[2 * g])
-                drain_pc(1, 2 * g + 1, pc[2 * g + 1])
-            else:
-                grouped = group_weight(last_raw, VECTOR_ROWS_LAST)
-            wq = quantize(work, "wt", grouped, E4M3, 2 if g == 2 else 1)
-            project(px, wq, x_q[g], E4M3, g == 0, g == 2)
-
-        result = [keep.tile([P, T], F32, name="result%d" % i) for i in range(N_TILES)]
-
-        def finish(i, t0, t1):
-            tok = slice(t0, t1)
-            bank = psum.tile([P, T], F32, name="bank")
-            k, ii = divmod(i, W_GROUP)
+            grouped = [group_weight(wc_raw[g][a], VECTOR_GROUPS) for a in range(2)]
             for a in range(2):
-                nc.tensor.matmul_mx(
-                    out=bank[:, tok],
-                    lhsT=w_codes[k][:, a, 2 * P * ii : 2 * P * (ii + 1)].bitcast(E2M1),
-                    lhsT_scale=w_plane[:, a, P * i : P * (i + 1)],
-                    rhs=h_codes[a][:, tok].bitcast(E4M3),
-                    rhs_scale=h_plane[a][:, tok],
-                    start=a == 0,
-                    stop=a == 1,
-                )
-            nc.scalar.activation(out=result[i][:, tok], in_=bank[:, tok], func=GELU, bias=bias[:, i : i + 1])
-            nc.sync.dma_start(out=out[i * P : (i + 1) * P, tok], in_=result[i][:, tok])
+                project(pc[a], quantize(work, "wt", grouped[a], E4M3), c_q[g], E5M2, g == 0, g == 1, plain)
 
-        multiply(1, 0, px[0])
-        multiply(1, 1, px[1])
+        x_q = []
+        for g in range(2):
+            x_q.append(quantize(keep, "x%d" % g, group_stream(x_raw[g], T), E4M3))
+            for q in range(QUARTERS):
+                drain_pc(g, q)
+        x_q.append(quantize(keep, "x2", group_stream(x_raw[2], VECTOR_TOKENS), E4M3))
+
+        px = [new_banks() for a in range(2)]
+        for a, g in ((0, 0), (1, 0), (0, 1), (0, 2)):
+            weight = quantize(work, "wt", group_weight(wx_raw[a, g], VECTOR_GROUPS), E4M3)
+            project(px[a], weight, x_q[g], E4M3, g == 0, g == 2, plain)
+        grouped = group_weight(wx_raw[1, 1], VECTOR_GROUPS_BUSY)
+        multiply(0, 0)
+        weight = quantize(work, "wt", grouped, E4M3)
+        multiply(0, 1)
+        project(px[1], weight, x_q[1], E4M3, False, False, plain)
+
+        grouped = work.tile([P, PASS, PACK], BF16, name="grouped", align_bytes=64)
+        group_columns(grouped, 0, last_raw[0][:], VECTOR_GROUPS_LAST[0])
+        quantize_h(0, 0, 2)
+        group_columns(grouped, P // 2, last_raw[1][:], VECTOR_GROUPS_LAST[1])
+        weight = quantize(work, "wt", grouped[:].rearrange("p n j -> p (n j)"), E4M3, 2)
+        project(px[1], weight, x_q[2], E4M3, False, True, urgent)
+        multiply(0, 2)
+        multiply(1, 0)
+        multiply(1, 1)
         quantize_h(1, 0, 1)
         quantize_h(1, 1, 2)
-        for i in range(EARLY_TILES):
-            finish(i, 0, T // 2)
-        multiply(1, 2, px[2])
-        multiply(1, 3, px[3])
+        finish(0, FIRST_HALF_STORES, slice(0, HALF), (0,))
+        multiply(0, 3)
+        multiply(1, 2)
+        quantize_h(0, 2, 4)
+        multiply(1, 3)
         quantize_h(1, 2, 3)
         quantize_h(1, 3, 4)
-        for i in range(EARLY_TILES):
-            finish(i, T // 2, T)
-        for i in range(EARLY_TILES, N_TILES):
-            finish(i, 0, T)
+        finish(0, SECOND_HALF_STORES, slice(HALF, T), (1, 0))
+        finish(sum(FIRST_HALF_STORES), WHOLE_STORES, slice(0, T), (1, 0))

from contextlib import ExitStack

import concourse.mybir as mybir
from concourse.masks import make_identity

K, L, R, M, T = 1536, 1024, 1024, 1536, 512
FLOPS = 2 * T * (K * R + L * R + R * M)

F32 = mybir.dt.float32
BF16 = mybir.dt.bfloat16
I32 = mybir.dt.int32
U32 = mybir.dt.uint32
U8 = mybir.dt.uint8
E4M3 = mybir.dt.float8_e4m3fn_x4
E5M2 = mybir.dt.float8_e5m2_x4
E2M1 = mybir.dt.float4_e2m1fn_x4
GELU = mybir.ActivationFunctionType.Gelu_apprx_tanh

P = 128
PACK = 4
PASS = P * PACK
QUARTER = 128
QUARTERS = T // QUARTER
HALF = T // 2
N_TILES = M // P
W_PARTS = (4, 8)
VECTOR_TOKENS = 320
VECTOR_GROUPS = 80
VECTOR_GROUPS_BUSY = 64
VECTOR_GROUPS_LAST = (24, 44)
FIRST_HALF_STORES = (1, 1, 2, 4)
SECOND_HALF_STORES = (4, 4)
WHOLE_STORES = (2, 1, 1)


def tile_mix_bilin_fm_gelu_kernel(tc, x, wx, c, wc, w_words, w_scales, b, out):
    nc = tc.nc
    with ExitStack() as ctx:
        keep = ctx.enter_context(tc.tile_pool(name="keep", bufs=1))
        work = ctx.enter_context(tc.tile_pool(name="work", bufs=3))
        psum = ctx.enter_context(tc.psum_pool(name="psum", bufs=4))
        ctx.enter_context(tc.manual_schedule())

        def load(name, src, g, col0, width):
            raw = keep.tile([P, PACK, width], F32, name=name)
            rows = src[g * PASS : (g + 1) * PASS, col0 : col0 + width]
            nc.sync.dma_start(out=raw[:], in_=rows.rearrange("(p j) n -> p j n", j=PACK))
            return raw

        def load_both_halves(name, src, g):
            raw = load(name, src, g, 0, R)
            return [raw[:, :, a * PASS : (a + 1) * PASS] for a in range(2)]

        b_rows = keep.tile([P, P], F32, name="b_rows")
        ident = keep.tile([P, P], F32, name="ident")
        bias = keep.tile([P, N_TILES], F32, name="bias")
        w_plane = keep.tile([P, 2, M], U8, name="w_plane", align_bytes=64)
        nc.vector.memset(b_rows[:], 0.0)
        nc.vector.memset(w_plane[:].bitcast(I32), 0)
        make_identity(nc, ident[:])

        c_raw = [load("c_raw%d" % g, c, g, 0, T) for g in range(2)]
        nc.sync.dma_start(out=b_rows[0:N_TILES, :], in_=b.rearrange("(i p) -> i p", p=P))
        wc_raw = [load_both_halves("wc_raw%d" % g, wc, g) for g in range(2)]
        x_raw = [load("x_raw%d" % g, x, g, 0, T) for g in range(3)]
        wx_first = load_both_halves("wx_raw0", wx, 0)
        wx_raw = {(a, 0): wx_first[a] for a in range(2)}
        for a, g in ((0, 1), (0, 2), (1, 1)):
            wx_raw[a, g] = load("wx_raw%d%d" % (a, g), wx, g, a * PASS, PASS)[:]
        last_raw = [load("last_raw%d" % s, wx, 2, PASS + s * PASS // 2, PASS // 2) for s in range(2)]
        for quad in range(4):
            nc.sync.dma_start(
                out=w_plane[32 * quad : 32 * quad + 4, :, :].bitcast(I32),
                in_=w_scales[:, 4 * quad : 4 * quad + 4, :].rearrange("a r n -> r a n").bitcast(I32),
            )
        w_codes = []
        for tiles in W_PARTS:
            first = len(w_codes)
            part = keep.tile([P, 2, 2 * P * tiles], U8, name="w_codes%d" % first, align_bytes=64)
            nc.sync.dma_start(
                out=part[:].bitcast(I32),
                in_=w_words[:, :, 2 * P * first : 2 * P * (first + tiles)].rearrange("a p n -> p a n").bitcast(I32),
            )
            w_codes.extend(part[:, :, 2 * P * i : 2 * P * (i + 1)] for i in range(tiles))

        def group_stream(raw, share):
            grouped = work.tile([P, T, PACK], BF16, name="grouped", align_bytes=64)
            dst = grouped[:].rearrange("p (n i) j -> p n j i", i=2)
            src = raw[:].rearrange("p j (n i) -> p n j i", i=2)
            nc.vector.tensor_copy(out=dst[:, 0 : share // 2], in_=src[:, 0 : share // 2])
            if share < T:
                nc.scalar.copy(out=dst[:, share // 2 :], in_=src[:, share // 2 :])
            return grouped[:].rearrange("p n j -> p (n j)")

        def group_columns(grouped, first, raw, share):
            src = raw.rearrange("p j (m t) -> p m j t", t=PACK)
            groups = src.shape[1]
            dst = grouped[:].rearrange("p (t m) j -> p m j t", t=PACK)[:, first : first + groups]
            for u in range(2):
                pair = slice(2 * u, 2 * u + 2)
                nc.vector.tensor_copy(out=dst[:, 0:share, :, pair], in_=src[:, 0:share, :, pair])
                nc.scalar.copy(out=dst[:, share:, :, pair], in_=src[:, share:, :, pair])

        def group_weight(raw, share):
            grouped = work.tile([P, PASS, PACK], BF16, name="grouped", align_bytes=64)
            group_columns(grouped, 0, raw, share)
            return grouped[:].rearrange("p n j -> p (n j)")

        def quantize(pool, name, grouped, fmt, calls=1):
            codes = pool.tile([P, PASS], U32, name=name + "_codes", align_bytes=64)
            plane = pool.tile([P, PASS], U8, name=name + "_plane", align_bytes=64)
            width = PASS // calls
            for u in range(calls):
                cols = slice(u * width, (u + 1) * width)
                nc.vector.quantize_mx(
                    out=codes[:, cols].bitcast(fmt),
                    scales=plane[:, cols],
                    in_=grouped[:, u * width * PACK : (u + 1) * width * PACK],
                )
            return codes, plane

        def project(banks, weight, stream, fmt, first, last, order):
            for q, t in order:
                tok = slice(q * QUARTER, (q + 1) * QUARTER)
                cols = slice(t * P, (t + 1) * P)
                nc.tensor.matmul_mx(
                    out=banks[q][:, cols],
                    lhsT=weight[0][:, cols].bitcast(E4M3),
                    lhsT_scale=weight[1][:, cols],
                    rhs=stream[0][:, tok].bitcast(fmt),
                    rhs_scale=stream[1][:, tok],
                    start=first and t == 0,
                    stop=last and t == PACK - 1,
                )

        plain = [(q, t) for q in range(QUARTERS) for t in range(PACK)]
        urgent = [(q, 2 * u + t) for u in range(2) for q in range(2) for t in range(2)] + plain[2 * PACK :]

        def new_banks():
            return [psum.tile([P, PASS], F32, name="bank%d" % (q // 2)) for q in range(QUARTERS)]

        pc_sb = [keep.tile([P, T * PACK], F32, name="pc_sb%d" % a) for a in range(2)]
        h_bf = [keep.tile([P, T * PACK], BF16, name="h_bf%d" % a, align_bytes=64) for a in range(2)]
        h_codes = [keep.tile([P, T], U32, name="h_codes%d" % a, align_bytes=64) for a in range(2)]
        h_plane = [keep.tile([P, T], U8, name="h_plane%d" % a, align_bytes=64) for a in range(2)]

        def drain_pc(a, q):
            nc.scalar.copy(
                out=pc_sb[a][:, q * PASS : (q + 1) * PASS].rearrange("p (n t) -> p n t", t=PACK),
                in_=pc[a][q][:].rearrange("p (t n) -> p n t", t=PACK),
            )

        def multiply(a, q):
            cols = slice(q * PASS, (q + 1) * PASS)
            nc.vector.tensor_tensor(
                out=h_bf[a][:, cols].rearrange("p (n t) -> p n t", t=PACK),
                in0=px[a][q][:].rearrange("p (t n) -> p n t", t=PACK),
                in1=pc_sb[a][:, cols].rearrange("p (n t) -> p n t", t=PACK),
                op=mybir.AluOpType.mult,
            )

        def quantize_h(a, q0, q1):
            tok = slice(q0 * QUARTER, q1 * QUARTER)
            nc.vector.quantize_mx(
                out=h_codes[a][:, tok].bitcast(E4M3),
                scales=h_plane[a][:, tok],
                in_=h_bf[a][:, q0 * PASS : q1 * PASS],
            )

        def finish(first, stores, tok, tags):
            width = tok.stop - tok.start
            for tiles in stores:
                result = keep.tile([P, tiles, width], F32, name="result%d_%d" % (first, tok.start))
                for i in range(first, first + tiles):
                    bank = psum.tile([P, PASS], F32, name="bank%d" % tags[i % len(tags)])
                    for a in range(2):
                        nc.tensor.matmul_mx(
                            out=bank[:, 0:width],
                            lhsT=w_codes[i][:, a, :].bitcast(E2M1),
                            lhsT_scale=w_plane[:, a, P * i : P * (i + 1)],
                            rhs=h_codes[a][:, tok].bitcast(E4M3),
                            rhs_scale=h_plane[a][:, tok],
                            start=a == 0,
                            stop=a == 1,
                        )
                    nc.scalar.activation(
                        out=result[:, i - first, :], in_=bank[:, 0:width], func=GELU, bias=bias[:, i : i + 1]
                    )
                rows = out[first * P : (first + tiles) * P, tok]
                nc.sync.dma_start(out=rows.rearrange("(i p) n -> p i n", p=P), in_=result[:])
                first += tiles

        c_q = [quantize(keep, "c%d" % g, group_stream(c_raw[g], VECTOR_TOKENS), E5M2) for g in range(2)]
        b_bank = psum.tile([P, PASS], F32, name="bank0")
        nc.tensor.transpose(b_bank[:, 0:P], b_rows[:], ident[:])
        nc.vector.tensor_copy(out=bias[:], in_=b_bank[:, 0:N_TILES])
        pc = [new_banks() for a in range(2)]
        for g in range(2):
            grouped = [group_weight(wc_raw[g][a], VECTOR_GROUPS) for a in range(2)]
            for a in range(2):
                project(pc[a], quantize(work, "wt", grouped[a], E4M3), c_q[g], E5M2, g == 0, g == 1, plain)

        x_q = []
        for g in range(2):
            x_q.append(quantize(keep, "x%d" % g, group_stream(x_raw[g], T), E4M3))
            for q in range(QUARTERS):
                drain_pc(g, q)
        x_q.append(quantize(keep, "x2", group_stream(x_raw[2], VECTOR_TOKENS), E4M3))

        px = [new_banks() for a in range(2)]
        for a, g in ((0, 0), (1, 0), (0, 1), (0, 2)):
            weight = quantize(work, "wt", group_weight(wx_raw[a, g], VECTOR_GROUPS), E4M3)
            project(px[a], weight, x_q[g], E4M3, g == 0, g == 2, plain)
        grouped = group_weight(wx_raw[1, 1], VECTOR_GROUPS_BUSY)
        multiply(0, 0)
        weight = quantize(work, "wt", grouped, E4M3)
        multiply(0, 1)
        project(px[1], weight, x_q[1], E4M3, False, False, plain)

        grouped = work.tile([P, PASS, PACK], BF16, name="grouped", align_bytes=64)
        group_columns(grouped, 0, last_raw[0][:], VECTOR_GROUPS_LAST[0])
        quantize_h(0, 0, 2)
        group_columns(grouped, P // 2, last_raw[1][:], VECTOR_GROUPS_LAST[1])
        weight = quantize(work, "wt", grouped[:].rearrange("p n j -> p (n j)"), E4M3, 2)
        project(px[1], weight, x_q[2], E4M3, False, True, urgent)
        multiply(0, 2)
        multiply(1, 0)
        multiply(1, 1)
        quantize_h(1, 0, 1)
        quantize_h(1, 1, 2)
        finish(0, FIRST_HALF_STORES, slice(0, HALF), (0,))
        multiply(0, 3)
        multiply(1, 2)
        quantize_h(0, 2, 4)
        multiply(1, 3)
        quantize_h(1, 2, 3)
        quantize_h(1, 3, 4)
        finish(0, SECOND_HALF_STORES, slice(HALF, T), (1, 0))
        finish(sum(FIRST_HALF_STORES), WHOLE_STORES, slice(0, T), (1, 0))
